import numpy as np, ml_dtypes
CORES = [51,54,179,182]
N = 4
BF = ml_dtypes.bfloat16
W, S, PA, TH, E, R = 3072, 128, 3, 112, 10, 5
def near(rng, pro, kin, amp):
    v = pro[np.arange(8)[None, :, None], kin]; v = v + rng.integers(-amp, amp + 1, v.shape)
    return np.ascontiguousarray(np.minimum(np.maximum(v, 0), 255).transpose(0, 1, 3, 2))
def parts(rng, ends=False):
    pro = rng.integers(0, 256, (8, 3, 16))
    x = near(rng, pro, rng.integers(0, 3, (N, 8, S)), E); d = near(rng, pro, rng.integers(0, 3, (N, 8, W)), E)
    d = np.where(rng.random((N, 8, 1, W)) < 0.25, rng.integers(0, 256, d.shape), d)
    key = rng.random((N, 8, R, W))
    if ends: key[..., 0] = -1.0; key[..., W - 1] = -1.0
    a = np.argsort(key, axis=-1)[..., :S]
    a = rng.permuted(a, axis=-1)
    b = rng.integers(0, W, (N, 8, R, S)); o = rng.integers(0, W, (N, 8, 16, S)); k = rng.integers(0, 2 * R, o.shape)
    for r in range(N):
        for t in range(R): o[r] = np.where(k[r] == t, a[(r + t) % N, :, t][:, None, :], o[r])
    h = np.where(rng.random((N, 8, W)) < 0.5, grantors(rng, a, W), rng.integers(0, W, (N, 8, W)))
    return x, d, o, h, a, b
def grantors(rng, a, n):
    return np.take_along_axis(a.reshape(N, 8, R * S), rng.integers(0, R * S, (N, 8, n)), 2)
def pack(x, d, o, h, a, b):
    return {"own": np.ascontiguousarray(o).reshape(N, 128, S).astype(np.int32), "lm": np.ascontiguousarray(x).reshape(N, 128, S).astype(np.float32).astype(BF),
            "bk": np.ascontiguousarray(d).reshape(N, 128, W).astype(np.float32).astype(BF), "heir": np.ascontiguousarray(h).astype(np.int32),
            "da": np.ascontiguousarray(a).reshape(N, 8, R * S).astype(np.int32), "db": np.ascontiguousarray(b).reshape(N, 8, R * S).astype(np.int32)}
def setup_inputs(rng):
    return pack(*parts(rng))
def setup_inputs_ties(rng):
    x, d, o, h, a, b = parts(rng); mid = rng.integers(60, 196, (8, 16)); x = x * 0 + mid[None, :, :, None]
    s = TH + rng.integers(-1, 2, (N, 8, 1, W)); v = s // 16 + (np.arange(16)[None, None, :, None] < s % 16)
    u = rng.integers(0, (TH - 1) // 16 + 1, (N, 8, 8, W)); v[:, :, :8] += u; v[:, :, 8:] -= u
    d = mid[None, :, :, None] + v * (1 - 2 * rng.integers(0, 2, v.shape))
    return pack(x, d, o, h, a, b)
def setup_inputs_wake(rng):
    x, d, o, h, a, b = parts(rng); pro = rng.integers(40, 216, (8, 1, 16))
    x = near(rng, pro, np.zeros((N, 8, S), np.int64), E // 2); d = rng.integers(0, 256, d.shape)
    o1 = grantors(rng, a, 16 * S).reshape(o.shape); o2 = np.roll(grantors(rng, a, 16 * S), -1, axis=0).reshape(o.shape)
    o = np.where(rng.random(o.shape) < 0.6, o1, o2); h = grantors(rng, a, W); b = np.roll(grantors(rng, a, R * S), -1, axis=0).reshape(b.shape)
    return pack(x, d, o, h, a, b)
def setup_inputs_sleep(rng):
    x, d, o, h, a, b = parts(rng); m = rng.permutation(8); g = m[0]
    a[:, g] = 2 * np.argsort(rng.random((N, W // 2)), axis=-1)[:, :R * S].reshape(N, R, S); x[:, g, :, ::8] = 0
    o[:, g] = 2 * rng.integers(0, W // 2, (N, 16, S)) + 1; h[:, g] = 2 * rng.integers(0, W // 2, (N, W)) + 1; b[:, g] = 2 * rng.integers(0, W // 2, (N, R, S)) + 1
    g = m[1]; a[:, g] = np.argsort(rng.random((N, R, S)), axis=-1)
    o[:, g] = rng.integers(S, W, (N, 16, S)); h[:, g] = rng.integers(S, W, (N, W)); b[:, g] = rng.integers(S, W, (N, R, S))
    nxt = np.roll(a, -1, axis=0)
    for g in m[2:4]:
        x[:, g] = rng.integers(155, 256, (N, 16, S)); d[:, g] = rng.integers(0, 101, (N, 16, W)); b[:, g, :R - 1] = nxt[:, g, 1:]
    o[:, m[2]] = a[:, m[2], 0][:, None, :]; o[:, m[3], 15] = a[:, m[3], 0]
    pro = rng.integers(0, 256, (8, 1, 16)); xn = near(rng, pro, np.zeros((N, 8, S), np.int64), E // 4); dn = near(rng, pro, np.zeros((N, 8, W), np.int64), E // 4)
    for g in m[4:6]:
        x[:, g] = xn[:, g]; d[:, g] = dn[:, g]; h[:, g] = (np.arange(W) + 1) % W
    for r in range(N):
        o[r, m[4]] = rng.permutation((W - 1 - np.arange(16 * S)) % W).reshape(16, S)
        o[r, m[5]] = W - 1 - (r % 2) * rng.integers(0, W // 4, (16, S))
    return pack(x, d, o, h, a, b)
def setup_inputs_alike(rng):
    x, d, o, h, a, b = parts(rng, True); c = 255 * rng.integers(0, 2, (8, 16))[None, :, :, None]; q = rng.permutation(N)
    x = x * 0 + c; x[..., 1::2] = 255 - x[..., 1::2]; x[q[0]] = c[0]
    v = np.where(rng.random((N, 8, 1, W)) < 0.5, c, 255 - c); v[q[0]] = c[0]
    two = rng.random((N, 8, 1, W)) < 0.25; two[q[0]] = False
    s = np.where(two, rng.choice(np.array([128, 160]), two.shape), rng.choice(np.array([0, TH, TH, TH + 1, TH + 1, 255]), two.shape))
    s[q[0]] = rng.choice(np.array([0, TH, TH]), (8, 1, W))
    i = rng.integers(0, 16, two.shape); j = (i + rng.choice(np.array([1, 2, 4, 8, 8]), two.shape)) % 16; p = np.arange(16)[None, None, :, None]
    one = (p == i) | (two & (p == j)); d = v + np.where(v == 0, s, -s) * one
    few = np.array([0, W - 1, W // 2, 3]); o[:, ::2] = rng.choice(few, (N, 4, 16, S))
    h = np.where(rng.random(h.shape) < 0.4, rng.choice(few, h.shape), h); b = np.where(rng.random(b.shape) < 0.3, rng.choice(few, b.shape), b)
    b[..., ::16] = a[..., ::16]; o[q[1], :, 5] = a[q[1], :, 0]
    return pack(x, d, o, h, a, b)
def setup_inputs_spread(rng):
    x, d, o, h, a, b = parts(rng); pro = (np.exp2(8 * rng.random((8, 3, 16))) - 1).astype(np.int64)
    x = near(rng, pro, (3 * rng.random((N, 8, S)) ** 2).astype(np.int64), rng.integers(0, 2 * E + 1, (N, 8, S, 1)))
    d = near(rng, pro, (3 * rng.random((N, 8, W)) ** 2).astype(np.int64), rng.integers(0, 2 * E + 1, (N, 8, W, 1)))
    o = np.where(rng.random(o.shape) < 0.5, (W * rng.random(o.shape) ** 3).astype(np.int64), o)
    h = (W * rng.random(h.shape) ** 3).astype(np.int64); b = (W * rng.random(b.shape) ** 3).astype(np.int64)
    return pack(x, d, np.minimum(o, W - 1), np.minimum(h, W - 1), a, np.minimum(b, W - 1))
def check_inputs(d):
    bad = []
    for k in ("own", "heir", "da", "db"):
        if np.min(d[k]) < 0 or np.max(d[k]) > W - 1: bad.append("range of " + k)
    for k in ("lm", "bk"):
        v = np.asarray(d[k]).astype(np.float32)
        if not np.all((v >= 0) & (v <= 255) & (v == np.floor(v))): bad.append("whole numbers from 0 to 255 in " + k)
    s = np.sort(np.asarray(d["da"]).reshape(N, 8, R, S), axis=-1)
    if np.any(s[..., 1:] == s[..., :-1]): bad.append("different grantors in a round of a rank and group")
    return bad
def reference(own, lm, bk, heir, da, db):
    o = own.astype(np.int64).reshape(N, 8, 16, S); x = lm.astype(np.float32).astype(np.int32).reshape(N, 8, 16, S)
    d = bk.astype(np.float32).astype(np.int32).reshape(N, 8, 16, W); h = heir.astype(np.int64)
    for t in range(R):
        for r in range(N):
            c = (r + t) % N
            a = da[c][:, t * S:(t + 1) * S].astype(np.int64); b = db[c][:, t * S:(t + 1) * S].astype(np.int64)
            hit = o[r] == a[:, None, :]
            o[r] = np.where(hit, b[:, None, :], o[r])
            g, i = np.nonzero(~np.any(hit, axis=1))
            d[c][g, :, a[g, i]] = x[r][g, :, i]
            h[c][g, a[g, i]] = b[g, i]
            for s in range(PA):
                e = o[r].reshape(8, 16 * S)
                w = np.take_along_axis(d[c], e[:, None, :], 2).reshape(8, 16, 16, S)
                dist = np.add.reduce(np.abs(w - x[r][:, :, None, :]), axis=1)
                o[r] = np.where(dist <= TH, np.take_along_axis(h[c], e, 1).reshape(8, 16, S), o[r])
    return {"yo": o.reshape(N, 128, S).astype(np.float32), "yd": d.reshape(N, 128, W).astype(np.float32).astype(BF), "yh": h.astype(np.float32)}

from concourse.mybir import AluOpType as ALU, ActivationFunctionType as ACT

W, R, NR = 3072, 5, 4
TH = 112
OPT = {"cut1": 40, "cut3": 32, "pre": True, "txq": "v", "tb": "vsvsvs", "ta": "svsvsv",
       "f": 1.25, "g": 1.56, "sct": 3.8, "pe": 0.5, "hop": 0.08, "far": 3.5, "slack": 0.2}
F, B, I, U = "float32", "bfloat16", "int32", "uint16"

SBUF = {
    "WN0": ([128, 4096], B), "WN1": ([128, 4096], B), "WA0": ([128, 4096], B), "WA1": ([128, 4096], B),
    "PK": ([128, 8, 1280], B),
    "GM0": ([128, 1024], B), "GM1": ([128, 1024], B), "GA0": ([128, 1024], B), "GA1": ([128, 1024], B),
    "OFF": ([128, 384], U), "DOF": ([128, 16], U), "RX": ([128, 640], F), "TX": ([128, 512], F),
    "M40": ([128, 256], F), "M41": ([128, 256], F), "E40": ([128, 256], F), "E41": ([128, 256], F),
    "SC0": ([128, 256], F), "SC1": ([128, 256], F), "HF": ([128, 256], F), "SG": ([128, 128], F),
    "HIT": ([128, 64], B), "HI2": ([128, 32], B), "TT": ([128, 64], F), "VM": ([128, 8], F), "AS": ([128, 256], B),
    "IO": ([128, 256], I), "IOF": ([128, 256], F), "TO": ([128, 8, 32], F), "LM": ([128, 4, 2, 16], B),
    "HB": ([128, 232], I), "HH": ([128, 232], B), "HL": ([128, 232], B),
    "HD": ([16, 3072], B), "BD": ([16, 5, 4, 2, 16], B),
    "EX": ([128, 64, 20], F), "AH": ([128, 4, 16], B), "AL": ([128, 4, 16], B), "Z": ([128, 128], F), "YO": ([128, 128], F),
    "ONE": ([128, 128], B), "J": ([128, 160], B), "KI": ([128, 4], I), "CI": ([128, 4], I), "CF": ([128, 12], F),
    "DUM": ([128, 8], F), "ID0": ([128, 160], B), "ID1": ([128, 160], B),
    "DUP": ([128, 256], B), "DUK": ([128, 256], B), "SEL": ([16, 256], B),
    "EM": ([128, 144], B), "ES": ([128, 144], B), "EH": ([128, 144], B), "PS": ([128, 128], B), "NI": ([128, 128], B),
}
SCRATCH = {k: ("sbuf", v[0], v[1]) for k, v in SBUF.items()}
SCRATCH.update({k: ("psum", [128, 512], F) for k in ("PH0", "PH1", "PD0", "PD1", "PV", "PX", "PG0", "PG1")})
SEMAPHORES = (["cv", "cs", "cp", "cg", "sent", "dhb", "dio", "dlm", "dbk0", "dbk1", "dhd", "dbd",
               "dyd0", "dyd1", "dyh0", "dyh1", "dyl0", "dyl1", "dyo"]
              + ["ao%d" % k for k in range(2, 10)] + ["ap%d" % k for k in range(2, 8)] + ["dx%d" % k for k in range(8)])
COUNTER = {"v": "cv", "s": "cs", "p": "cp", "g": "cg"}
X0, XS, SH, SL = 512, 1024, 1152, 1216


def rank_program(g, core, T, topo):
    rank = T.rank_of(core)
    if rank is None:
        return
    cores = list(T.cores)
    common = [e for e in topo.engines(cores[0], cores[1])
              if all(e in topo.engines(a, b) for a in cores for b in cores if a != b)]
    mask = sum(1 << e for e in common)
    ne = len(common)
    queue = {"v": g.vector, "s": g.scalar, "p": g.tensor, "g": g, "y": g.sync}

    ops, writer, readers, bank, group = [], {}, {}, {}, {}
    cyc = 0.00083 * OPT["f"]

    def op(q, fn, cost, r=(), w=(), ps=(), sem=None, lat=0.0):
        me = len(ops)
        deps = {}
        for k in r:
            if k in writer:
                deps[writer[k]] = True
        for k in w:
            for d in ([writer[k]] if k in writer else []) + readers.get(k, []):
                deps[d] = True
        for k in ps:
            last, run, before = bank.get(k, (None, [], []))
            if last != q:
                run, before = [], run
            for d in before + (run if k in w else []):
                deps[d] = True
            if q == "p" and run:
                deps.setdefault(run[-1], False)
                if run[-1] == me - 1 and all(d == me - 1 or d in ops[me - 1]["deps"] for d in deps):
                    ops[me - 1]["fn"].append(fn)
                    ops[me - 1]["cost"] += cost
                    for j in r:
                        readers.setdefault(j, []).append(me - 1)
                    return me - 1
            bank[k] = (q, ([] if q == "p" else run) + [me], before)
        ops.append({"q": q, "fn": [fn], "deps": deps, "cost": cost, "lat": lat, "sem": sem})
        if sem is not None:
            group.setdefault(sem[0], []).append(me)
        for k in r:
            readers.setdefault(k, []).append(me)
        for k in w:
            writer[k] = me
            readers[k] = []
        return me

    def dma(q, out, in_, r, w, sem, kb=32, **kw):
        op(q, lambda: queue[q].dma_start(out, in_, **kw), 1.0 if q == "g" else 0.1, r, w, sem=(sem, 16), lat=2.0 + kb / 200.0)

    landing = {}

    def send(dst, out, in_, r, sem, kb):
        rid, pid = topo.addr(dst, core)
        me = op("g", lambda: g.remote_dma(out, in_, T.sem[sem], T.sem.sent, pid, rid, mask), 0.3, r, (), sem=("sent", ne))
        ops[landing[sem]]["deps"][me] = False
        ops[landing[sem]]["lat"] = OPT["far"] + kb / 60.0

    def lands(keys, sem):
        landing[sem] = op(None, None, 0.0, (), keys, sem=(sem, ne))

    def vcost(n, kind=""):
        if kind == "gather":
            return 0.05 * OPT["f"] + n * OPT["g"] * cyc
        if kind == "scatter":
            return 0.05 * OPT["f"] + n * OPT["sct"] * cyc
        return max(64, n) * cyc

    def act(out, in_, fn, r, w, ps=(), n=64, kind="", **kw):
        op("s", lambda: g.scalar.activation(out, in_, fn, **kw), 0.065 * OPT["f"] + n * cyc * (OPT["g"] if kind else 1), r, w, ps)

    def copy(q, out, in_, r, w, ps=(), n=64, kind=""):
        if q == "v":
            op("v", lambda: g.vector.tensor_copy(out, in_), vcost(n, kind), r, w, ps)
        elif q == "s":
            act(out, in_, ACT.Identity, r, w, ps, n)
        else:
            op("g", lambda: g.affine_select(out, in_, [[0, n]], ALU.is_gt, 0.0, 1, 0), 0.2 + 2 * n * cyc, r, w, ps)

    def tt(out, a, b, alu, r, w, ps=(), n=64, kind=""):
        op("v", lambda: g.vector.tensor_tensor(out, a, b, alu), vcost(n if ps or kind else 2 * n, kind), r, w, ps)

    def ts(out, a, s1, s2, o0, o1, r, w, ps=(), n=64):
        if o1 is None:
            op("v", lambda: g.vector.tensor_scalar(out, a, s1, None, o0), vcost(n), r, w, ps)
        else:
            op("v", lambda: g.vector.tensor_scalar(out, a, s1, s2, o0, o1), vcost(n), r, w, ps)

    def mm(out, lhs, rhs, start, stop, r, ps, n=64):
        op("p", lambda: g.tensor.matmul(out, lhs, rhs, start, stop), n * OPT["pe"] * cyc, r, (), [ps])

    def fill(ap, c, w):
        op("v", lambda: g.vector.memset(ap, c), vcost(128), (), w)

    def gop(fn, n, r, w):
        op("g", fn, 0.2 + 2 * n * cyc, r, w)

    WN, WA = [T.WN0, T.WN1], [T.WA0, T.WA1]
    GM, GA = [T.GM0, T.GM1], [T.GA0, T.GA1]
    M4, E4, SC = [T.M40, T.M41], [T.E40, T.E41], [T.SC0, T.SC1]
    IDS, PG = [T.ID0, T.ID1], [T.PG0, T.PG1]
    PH, PD = [T.PH0, T.PH1], [T.PD0, T.PD1]
    for s in range(2, 10):
        lands(["RX%d" % s], "ao%d" % s)
    for s in range(2, 8):
        lands(["PK%s%d" % (part, s) for part in "XSD"], "ap%d" % s)

    def book(q, y, after):
        for a in range(4):
            for h in range(2):
                dma(q, WN[y][32 * a + 16 * h:32 * a + 16 * h + 16, 0:W], T.bk[32 * a + 16 * y:32 * a + 16 * y + 16, :],
                    after, ["WN%d.%d" % (y, 2 * a + h)], "dbk%d" % y, kb=400)

    def wn_keys(y):
        return ["WN%d.%d" % (y, j) for j in range(8)]

    def wa_keys(y):
        return ["WA%d.%d" % (y, j) for j in range(6)]

    inkeys = ["INa%d" % a for a in range(4)] + ["INb%d" % a for a in range(4)]
    fill(T.IO[:, 128:256], 0, inkeys)
    fill(T.ONE[:], 1.0, ["ONE"])
    gop(lambda: g.iota(T.KI[:, 0:1], [[0, 1]], 0, 1), 1, (), ["KI"])
    gop(lambda: g.iota(T.J[:], [[1, 160]], 0, -1, allow_small_or_imprecise_dtypes=True), 160, (), ["J"])
    dma("y", T.HB[:, 0:192], T.heir[:], (), ["HBh"], "dhb")
    dma("y", T.HB[:, 192:232], T.db[:], (), ["HBb"], "dhb")
    dma("y", T.IO[:, 0:128], T.own[:], (), ["OWN"], "dio")
    dma("s", T.LM[:], T.lm[:], (), ["LM"], "dlm")
    book("s", 0, ())
    for a in range(4):
        dma("y", T.IO[32 * a:32 * a + 10, 128:256], T.da[2 * a:2 * a + 2, :], (), ["INa%d" % a], "dio")
    for a in range(4):
        dma("y", T.IO[32 * a + 16:32 * a + 26, 128:256], T.db[2 * a:2 * a + 2, :], (), ["INb%d" % a], "dio")

    fill(T.SEL[:], 0.0, ["SEL0", "SEL1"])
    for y in range(2):
        gop(lambda y=y: g.affine_select(T.DUP[:, 128 * y:128 * y + 128], T.ONE[:], [[-32, 4], [0, 2], [-1, 16]],
                                        ALU.is_equal, 0.0, -16 * y, 1), 128, ["ONE"], ["DUP%d" % y])
    gop(lambda: g.iota(T.DUM[:], [[1, 8]], W, 8, allow_small_or_imprecise_dtypes=True), 8, (), ["DUM"])
    for y in range(2):
        for d in range(2):
            gop(lambda y=y, d=d: g.affine_select(T.SEL[:, 128 * y + 8 + d:128 * y + 128:16], T.ONE[0:16, 0:8], [[-2, 4], [0, 2]],
                                                 ALU.is_equal, 0.0, -8 * d - y, 1), 8, ["ONE"], ["SEL%d" % y])
    ts(T.CI[:, 0:1], T.KI[:, 0:1], 4, 1, ALU.logical_shift_right, ALU.bitwise_and, ["KI"], ["CI0"])
    ts(T.CI[:, 1:2], T.KI[:, 0:1], 3, 1, ALU.logical_shift_right, ALU.bitwise_and, ["KI"], ["CI1"])
    ts(T.CI[:, 2:3], T.KI[:, 0:1], 15, None, ALU.bitwise_and, None, ["KI"], ["CI2"])
    fill(T.M40[:, 0::4], 0.0, ["M40"])
    fill(T.M41[:, 0::4], 0.0, ["M41"])
    copy("v", T.CF[:, 0:3], T.CI[:, 0:3], ["CI0", "CI1", "CI2"], ["CF"])
    ts(T.CF[:, 4:6], T.CF[:, 0:2], -1.0, 1.0, ALU.mult, ALU.add, ["CF"], ["CF4"])
    ts(T.CF[:, 6:7], T.CF[:, 2:3], -1.0, 15.0, ALU.mult, ALU.add, ["CF"], ["CF6"])
    ts(T.CF[:, 7:8], T.CF[:, 1:2], -8.0, None, ALU.mult, None, ["CF"], ["CF7"])
    ts(T.CF[:, 8:9], T.CF[:, 1:2], -256.0, 256.0, ALU.mult, ALU.add, ["CF"], ["BIAS"])
    ts(T.ID0[:], T.J[:], 16.0, T.CF[:, 4:5], ALU.is_equal, ALU.mult, ["J", "CF4"], ["ID0"])
    ts(T.ID1[:], T.J[:], 16.0, T.CF[:, 0:1], ALU.is_equal, ALU.mult, ["J", "CF"], ["ID1"])
    ts(T.PS[:], T.J[:, 0:128], T.CF[:, 7:8], -1.0, ALU.is_equal, ALU.mult, ["J", "CF7"], ["PS"])
    ts(T.EM[:], T.J[:, 0:144], T.CF[:, 6:7], 2.0, ALU.is_equal, ALU.mult, ["J", "CF6"], ["EM"])
    ts(T.ES[:], T.J[:, 0:144], T.CF[:, 6:7], T.CF[:, 5:6], ALU.is_equal, ALU.mult, ["J", "CF6", "CF4"], ["ES"])
    ts(T.EH[:], T.J[:, 0:144], T.CF[:, 6:7], T.CF[:, 1:2], ALU.is_equal, ALU.mult, ["J", "CF6", "CF"], ["EH"])
    ts(T.NI[:], T.J[:, 0:128], 0.0, -0.5, ALU.is_equal, ALU.mult, ["J"], ["NI"])
    ts(T.DUK[:], T.DUP[:], 4096.0, None, ALU.mult, None, ["DUP0", "DUP1"], ["DUK"], n=128)
    bias = T.CF[:, 8:9]

    copy("v", T.HH[:], T.HB[:], ["HBh", "HBb"], ["HH"], n=232)
    tt(T.HL[:], T.HB[:], T.HH[:], ALU.subtract, ["HBh", "HBb", "HH"], ["HL"], n=232)
    dma("y", T.HD[0:8, :], T.HH[:, 0:192], ["HH"], ["HD0"], "dhd")
    dma("y", T.BD[0:8], T.HH[:, 192:232], ["HH"], ["BD0"], "dbd")
    dma("y", T.HD[8:16, :], T.HL[:, 0:192], ["HL"], ["HD1"], "dhd")
    dma("y", T.BD[8:16], T.HL[:, 192:232], ["HL"], ["BD1"], "dbd")

    def xtile(y):
        for j in range(8):
            for h in range(2):
                o = 16 + 16 * y - 16 * h
                mm(PG[y][:, 64 * j:64 * j + 64], IDS[y][:, o:o + 128], T.LM[:, :, h, :], h == 0, h == 1,
                   ["ID%d" % y, "LM"], "PG%d" % y)
        copy("s", T.PK[:, y, X0:XS], PG[y][:], (), ["PKX%d" % y], ["PG%d" % y], n=512)

    def widen(s):
        dma("y", T.PK[:, s, 0:X0], T.PK[:, s, X0:XS], ["PKX%d" % s], ["PKW%d" % s], "dx%d" % s, kb=128)
    xtile(0)
    for y in range(2):
        for h in range(2):
            mm(T.PX[:, 128 * y + 64 * h:128 * y + 64 * h + 64], T.DUP[:, 128 * y:128 * y + 128], T.LM[:, :, h, :],
               True, True, ["DUP%d" % y, "LM"], "PX")
    copy("s", T.PK[:, 0:2, XS:SH], T.PX[:, 0:256], (), ["PKS0", "PKS1"], ["PX"], n=256)
    xtile(1)
    widen(0)
    book("y", 1, ["HL", "PKX0", "WN0.0"])
    widen(1)

    def landmark_sums():
        for y in range(2):
            for p in range(16):
                mm(T.PV[:, 64 + 32 * y:96 + 32 * y], T.EM[:, 15 - p:143 - p], T.PK[:, y, X0 + p:XS:16], p == 0, p == 15,
                   ["EM", "PKX%d" % y], "PV")
        for j in range(2):
            copy("s", T.PK[:, 0:2, SH + 32 * j:SH + 32 * j + 32], T.PV[:, 64:128], (), ["PKh%d" % j], ["PV"])
        for j in range(2):
            tt(T.PK[:, 0:2, SL + 32 * j:SL + 32 * j + 32], T.PV[:, 64:128], T.PK[:, 0:2, SH:SH + 32], ALU.subtract,
               ["PKh0", "PKh1"], ["PKl%d" % j] + (["PKD0", "PKD1"] if j else []), ["PV"])

    copy("v", T.IOF[:], T.IO[:], inkeys + ["OWN"], ["IOF"], n=256)
    op("v", lambda: g.vector.transpose(T.TO[:], T.IOF[:]), vcost(256), ["IOF"], ["TO"])
    tt(T.EX[:, 0:4, 10:20], T.TO[:, 4:8, 16:26], T.TO[:, 4:8, 0:10], ALU.subtract, ["TO"], ["EXb"])
    copy("v", T.AH[:, :, 0:10], T.TO[:, 4:8, 0:10], ["TO"], ["AH"])

    def aux_source(t, y):
        s = 2 * (t % NR) + y
        for h in range(2):
            o = T.PX[:, 256 + 64 * h:256 + 64 * h + 64]
            mm(o, T.PS[:], T.PK[:, s, XS + 64 * h:XS + 64 * h + 64], True, False, ["PS", "PKS%d" % s], "PX")
            mm(o, T.SEL[:, 128 * y:128 * y + 128], T.BD[:, t, :, h, :], False, True, ["SEL%d" % y, "BD0", "BD1"], "PX")

    def aux_source_copy(y):
        act(T.AS[:, 128 * y:128 * y + 128], T.PX[:, 256:384], ACT.Identity, ["BIAS"], ["AS%d" % y], ["PX"], 128, bias=bias)

    exk = ["EXa", "EXb", "EX4", "EX8", "EX16", "EX32"]

    def stage(t, y):
        copy("s", PG[y][:, 0:128], T.EX[:, :, 5 * y + t::10], exk, ["PG%d" % y], ["PG%d" % y], n=128)

    def rx_keys(t, y):
        return ["RX1.%d" % b for b in range(4)] if t == 0 else ["RX%d" % (2 * t + y)]

    def deed_hit(t, y):
        s = 2 * t + y
        if t > 0:
            tt(T.HIT[:], T.RX[:, 64 * s:64 * s + 64], PG[y][:, 0:128:2], ALU.is_equal, rx_keys(t, y), ["HIT"], ["PG%d" % y])
        else:
            tt(T.HIT[:], T.RX[:, 64 * s:64 * s + 64], T.EX[:, :, 5 * y + t], ALU.is_equal, rx_keys(t, y) + exk, ["HIT"])

    def deed_pre(keys=("HIT",)):
        if OPT["pre"]:
            tt(T.HI2[:], T.HIT[:, 0:32], T.HIT[:, 32:64], ALU.add, list(keys), ["HI2"], n=32)

    def deed_count(t, y, keys=("HIT",)):
        src, nq, keys = (T.HI2, 8, ["HI2"]) if OPT["pre"] else (T.HIT, 16, list(keys))
        for h in range(2):
            o = T.PV[:, 4 * h:4 * h + 4]
            dup = T.DUP[:, 128 * h:128 * h + 128]
            mm(o, dup, T.AH[:, :, 5 * y + t], True, False, ["DUP%d" % h, "AH"], "PV")
            mm(o, dup, T.AL[:, :, 5 * y + t], False, False, ["AL"], "PV")
            for q in range(nq):
                mm(o, T.DUK[:, 128 * h:128 * h + 128], src[:, 4 * q:4 * q + 4], False, q == nq - 1, ["DUK"] + keys, "PV")

    def deed_step(t, y):
        if t > 0:
            tt(PG[y][:, 128:192], T.HIT[:], PG[y][:, 1:128:2], ALU.mult, ["HIT"], ["TT"], ["PG%d" % y])
        else:
            tt(T.TT[:], T.HIT[:], T.EX[:, :, 10 + 5 * y + t], ALU.mult, ["HIT"] + exk, ["TT"])

    def deed_owners(t, y):
        s = 2 * t + y
        if t > 0:
            tt(E4[y][:, 3::4], T.RX[:, 64 * s:64 * s + 64], PG[y][:, 128:192], ALU.add, rx_keys(t, y) + ["TT"], ["E4%d.3" % y],
               ["PG%d" % y])
        else:
            tt(E4[y][:, 3::4], T.RX[:, 64 * s:64 * s + 64], T.TT[:], ALU.add, rx_keys(t, y) + ["TT"], ["E4%d.3" % y])

    def first_list(y, keys=None):
        copy("v", T.OFF[:, 192 * y:192 * y + 64], E4[y][:, 3::4], keys or ["E4%d.3" % y], ["OFF%d.0" % y])

    def deed_min():
        tt(T.VM[:], T.PV[:, 0:8], T.DUM[:], ALU.min, ["DUM"], ["VM"], ["PV"])

    def deed_list(y):
        copy("v", T.DOF[:, 8 * y:8 * y + 8], T.VM[:], ["VM"], ["DOF%d" % y])

    def sleep_aux(y):
        copy("v", WA[y][:, 0:4096].indirect(T.DOF[:, 8 * y:8 * y + 8]), T.AS[:, 128 * y:128 * y + 128],
             ["DOF%d" % y, "AS%d" % y], wa_keys(y), n=128, kind="scatter")

    def sleep_num(t, y):
        s = 2 * (t % NR) + y
        copy("v", WN[y][:, 0:4096].indirect(T.DOF[:, 8 * y:8 * y + 8]), T.PK[:, s, XS:SH], ["DOF%d" % y, "PKS%d" % s],
             wn_keys(y), n=128, kind="scatter")

    def gather_s(y, k, n):
        o = 192 * y + 64 * k
        act(GA[n % 2][:], WA[y][:, 0:W].indirect(T.OFF[:, o:o + 64]), ACT.Identity,
            wa_keys(y) + ["OFF%d.%d" % (y, k)], ["GA%d" % (n % 2)], n=1024, kind="gather")

    def gather_v(t, y, k, n, half=None, cut=32):
        s = 2 * (t % NR) + y
        c0, c1 = (0, 64) if half is None else ((0, cut) if half == 0 else (cut, 64))
        o, m = 192 * y + 64 * k, 16 * (c1 - c0)
        tt(GM[n % 2][:, 16 * c0:16 * c1], WN[y][:, 0:W].indirect(T.OFF[:, o + c0:o + c1]), T.PK[:, s, XS - m:XS], ALU.max,
           wn_keys(y) + ["OFF%d.%d" % (y, k), "PKX%d" % s] + (["PKW%d" % s] if m > 512 else []),
           ["GM%d.%d" % (n % 2, hf) for hf in ([0, 1] if half is None else [half])], n=m, kind="gather")

    def sum_heir(n):
        for p in range(16):
            mm(PH[n % 2][:, 0:64], T.EH[:, 15 - p:143 - p], GA[n % 2][:, p::16], p == 0, p == 15,
               ["EH", "GA%d" % (n % 2)], "PH%d" % (n % 2))

    def sum_pairs(t, y, n):
        s = 2 * (t % NR) + y
        o, key = PD[n % 2][:, 0:64], "PD%d" % (n % 2)
        mm(o, T.NI[:], T.PK[:, s, SH:SL], True, False, ["NI", "PKD%d" % s] + (["PKl0"] if s < 2 else []), key)
        mm(o, T.NI[:], T.PK[:, s, SL:SL + 64], False, False, (), key)
        for p in range(16):
            mm(o, T.ES[:, 15 - p:143 - p], GA[n % 2][:, p::16], False, False, ["ES", "GA%d" % (n % 2)], key)

    def sum_max(n):
        o, key = PD[n % 2][:, 0:64], "PD%d" % (n % 2)
        for p in range(16):
            mm(o, T.EM[:, 15 - p:143 - p], GM[n % 2][:, p::16], False, p == 15,
               ["EM", "GM%d.0" % (n % 2), "GM%d.1" % (n % 2)], key)

    def next_list(y, k, n):
        o = 192 * y + 64 * (k + 1)
        copy("v", T.OFF[:, o:o + 64], PH[n % 2][:, 0:64], (), ["OFF%d.%d" % (y, k + 1)], ["PH%d" % (n % 2)])

    def delta(y, k, n):
        if k == 0:
            prev, key = E4[y][:, 3::4], "E4%d.3" % y
        else:
            o = 128 * y + 64 * (k - 1)
            prev, key = T.HF[:, o:o + 64], "HF%d.%d" % (y, k - 1)
        tt(E4[y][:, 2 - k::4], PH[n % 2][:, 0:64], prev, ALU.subtract, [key], ["E4%d.%d" % (y, 2 - k)], ["PH%d" % (n % 2)])

    def keep_heir(y, k, n):
        o = 128 * y + 64 * k
        copy("s", T.HF[:, o:o + 64], PH[n % 2][:, 0:64], (), ["HF%d.%d" % (y, k)], ["PH%d" % (n % 2)])

    def near_sign(k, n):
        act(T.SG[:, 64 * k:64 * k + 64], PD[n % 2][:, 0:64], ACT.Sign, (), ["SG%d" % k], ["PD%d" % (n % 2)],
            bias=TH + 2048.5, scale=-1.0)

    def near_mask(y, k):
        act(M4[y][:, 3 - k::4], T.SG[:, 64 * k:64 * k + 64], ACT.Relu, ["SG%d" % k], ["M4%d" % y])

    def landmarks_to(t, y, after):
        s = 2 * t + y
        send(cores[(rank + t) % NR], T.PK[:, s, X0:], T.PK[:, y, X0:],
             ["PKX%d" % y, "PKS%d" % y, "PKD%d" % y, "PKl0"] + after, "ap%d" % s, 192)

    def tail_a(y, n):
        delta(y, 2, n)
        ts(M4[y][:, 1::4], PD[n % 2][:, 0:64], TH + 2048.5, None, ALU.is_le, None, (), ["M4%d" % y], ["PD%d" % (n % 2)])

    def tail_b(t, y):
        op("v", lambda: g.vector.tensor_tensor_scan(SC[y][:], M4[y][:], E4[y][:], 0.0, ALU.mult, ALU.add), vcost(256),
           ["M4%d" % y] + ["E4%d.%d" % (y, j) for j in range(4)], ["SC%d" % y])
        if t < R - 1:
            s = 2 * t + y
            copy(OPT["txq"], T.TX[:, 64 * s:64 * s + 64], SC[y][:, 3::4], ["SC%d" % y], ["TX%d" % s])
            send(cores[(rank + 1) % NR], T.RX[:, 64 * (s + 2):64 * (s + 3)], T.TX[:, 64 * s:64 * s + 64], ["TX%d" % s],
                 "ao%d" % (s + 2), 32)
            if t + 2 < NR:
                landmarks_to(t + 2, y, ["TX%d" % s])
        else:
            for b in range(4):
                copy("v" if (y == 1 and b % 2 == 0) else "s", T.Z[:, 32 * b + 16 * y:32 * b + 16 * y + 16], SC[y][:, 4 * b + 3::16],
                     ["SC%d" % y], ["Z%d.%d" % (y, b)], n=16)

    def books_out(y):
        for a in range(4):
            dma("y", T.yd[32 * a + 16 * y:32 * a + 16 * y + 16, :], WN[y][32 * a:32 * a + 16, 0:W],
                wn_keys(y) + ["RX%d" % (2 * R - 1)], (), "dyd%d" % y, kb=200)
        dma("g", T.yh[y::2, :], WA[y][8::32, 0:W], wa_keys(y) + ["TX%d" % (2 * R - 3)], ["yh%d" % y], "dyh%d" % y)
        dma("g", T.yh[y::2, :], WA[y][9::32, 0:W], wa_keys(y), ["yh%d" % y], "dyl%d" % y, accum_op=ALU.add, max_dma_last_dim=4096)

    def table_pairs(y, c, pb):
        mm(T[pb][:], T.PS[:], WN[y][:, 512 * c:512 * c + 512], True, False, ["PS"] + wn_keys(y), pb, 512)

    def table_heirs(y, c, pb):
        mm(T[pb][:], T.SEL[:, 128 * y:128 * y + 128], T.HD[:, 512 * c:512 * c + 512], False, True,
           ["SEL%d" % y, "HD0", "HD1"], pb, 512)

    def table_copy(q, y, c, pb):
        cs = slice(512 * c, 512 * c + 512)
        if q == "v":
            ts(WA[y][:, cs], T[pb][:], bias, None, ALU.add, None, ["BIAS"], ["WA%d.%d" % (y, c)], [pb], 512)
        else:
            act(WA[y][:, cs], T[pb][:], ACT.Identity, ["BIAS"], ["WA%d.%d" % (y, c)], [pb], 512, bias=bias)

    hits = ["HIT%d" % b for b in range(4)]
    for b in range(4):
        ts(T.HIT[:, b::4], T.TO[:, b, 0:16], T.TO[:, 4 + b, 0:1], None, ALU.is_equal, None, ["TO"], [hits[b]])
    tt(T.AL[:, :, 0:10], T.TO[:, 4:8, 0:10], T.AH[:, :, 0:10], ALU.subtract, ["TO", "AH"], ["AL"])
    deed_pre(hits)
    deed_count(0, 0, hits)
    for b in range(4):
        ts(T.TT[:, 16 * b:16 * b + 16], T.TO[:, b, 0:16], T.TO[:, 4 + b, 0:1], T.EX[:, b, 10:11], ALU.is_equal, ALU.mult,
           ["TO", "EXb"], ["TT%d" % b])
    for b in range(4):
        tt(T.E40[:, 4 * b + 3::16], T.TO[:, b, 0:16], T.TT[:, 16 * b:16 * b + 16], ALU.add, ["TO", "TT%d" % b], ["E4b%d" % b], n=16)
    deed_min()
    first_list(0, ["E4b%d" % b for b in range(4)])
    writer["E40.3"] = writer["OFF0.0"]
    writer["HIT"], readers["HIT"] = writer["HIT3"], list(readers["HIT3"])
    writer["TT"] = writer["OFF0.0"]
    deed_list(0)
    copy("g", T.EX[:, 0:4, 0:10], T.TO[:, 4:8, 0:10], ["TO"], ["EXa"], n=40)
    for b in range(4):
        copy("g", T.RX[:, 64 + b:128:4], T.TO[:, b, 16:32], ["TO"], ["RX1.%d" % b], n=16)
    for j, m in enumerate((4, 8, 16, 32)):
        copy("g", T.EX[:, m:2 * m, :], T.EX[:, 0:m, :], exk[:2 + j], ["EX%d" % m], n=20 * m)
    banks = ["PH0", "PH1", "PD0", "PD1", "PG1", "PG0"]
    for c in range(6):
        table_pairs(0, c, banks[c])
    aux_source(0, 0)
    aux_source_copy(0)
    sleep_num(0, 0)
    for c in range(6):
        table_heirs(0, c, banks[c])
        table_copy(OPT["ta"][c], 0, c, banks[c])
    sleep_aux(0)
    landmark_sums()
    landmarks_to(1, 0, [])
    landmarks_to(1, 1, [])
    for s in range(2, 8):
        widen(s)

    def table1(c):
        table_pairs(1, c, banks[4 + c % 2])
        table_heirs(1, c, banks[4 + c % 2])
        table_copy(OPT["tb"][c], 1, c, banks[4 + c % 2])

    turns = [(t, y) for t in range(R) for y in range(2)]
    for j, (t, y) in enumerate(turns):
        n = 3 * j
        nxt = turns[j + 1] if j + 1 < len(turns) else None
        gather_s(y, 0, n)
        if j > 0:
            sleep_num(t, y)
            tail_a(1 - y, n - 1)
            tail_b(turns[j - 1][0], 1 - y)
        if t == R - 1:
            books_out(y)
        if nxt:
            aux_source(*nxt)
        sum_heir(n)
        if nxt:
            aux_source_copy(nxt[1])
            if j > 0:
                stage(*nxt)
        if j == 0:
            table1(0)
            table1(1)
        gather_v(t, y, 0, n, 0, OPT["cut1"])
        next_list(y, 0, n)
        gather_s(y, 1, n + 1)
        gather_v(t, y, 0, n, 1, OPT["cut1"])
        sum_pairs(t, y, n)
        sum_max(n)
        delta(y, 0, n)
        if j == 0:
            table1(2)
        sum_heir(n + 1)
        sum_pairs(t, y, n + 1)
        keep_heir(y, 0, n)
        if j == 0:
            table1(3)
        near_sign(0, n)
        gather_v(t, y, 1, n + 1)
        next_list(y, 1, n + 1)
        gather_s(y, 2, n + 2)
        sum_max(n + 1)
        delta(y, 1, n + 1)
        near_mask(y, 0)
        if j == 0:
            table1(4)
            table1(5)
        if nxt:
            gather_v(t, y, 2, n + 2, 0, OPT["cut3"])
            deed_hit(*nxt)
            deed_pre()
            deed_count(*nxt)
            gather_v(t, y, 2, n + 2, 1, OPT["cut3"])
        else:
            gather_v(t, y, 2, n + 2)
        keep_heir(y, 1, n + 1)
        near_sign(1, n + 1)
        near_mask(y, 1)
        sum_heir(n + 2)
        sum_pairs(t, y, n + 2)
        sum_max(n + 2)
        if nxt:
            deed_step(*nxt)
            deed_min()
            deed_owners(*nxt)
            deed_list(nxt[1])
            first_list(nxt[1])
            sleep_aux(nxt[1])
    tail_a(1, 3 * len(turns) - 1)
    tail_b(R - 1, 1)
    op("v", lambda: g.vector.transpose(T.YO[:], T.Z[:]), vcost(128), ["Z%d.%d" % (y, b) for y in range(2) for b in range(4)], ["YO"])
    dma("y", T.yo[:], T.YO[:], ["YO"], (), "dyo")

    for o in ops:
        for d in list(o["deps"]):
            sem = ops[d]["sem"]
            if sem is not None and sem[0] != "sent":
                for e in group[sem[0]]:
                    o["deps"][e] = True
    succ = [[] for _ in ops]
    left = [len(o["deps"]) for o in ops]
    for i, o in enumerate(ops):
        for d in o["deps"]:
            succ[d].append(i)
    ready = {q: [] for q in list(queue) + [None]}
    at, free, order = [0.0] * len(ops), {q: 0.0 for q in ready}, []
    for i in range(len(ops)):
        if left[i] == 0:
            ready[ops[i]["q"]].append(i)
    while len(order) < len(ops):
        best = None
        for q, lst in ready.items():
            if not lst:
                continue
            lst.sort()
            a = lst[0]
            if q is not None:
                limit = 1e9
                for b in lst:
                    tb = max(at[b], free[q])
                    if tb + ops[b]["cost"] <= limit + OPT["slack"] and tb < max(at[a], free[q]):
                        a = b
                    limit = min(limit, tb)
            t0 = max(at[a], free[q])
            if best is None or t0 < best[0]:
                best = (t0, a)
        t0, i = best
        o = ops[i]
        ready[o["q"]].remove(i)
        order.append(i)
        if o["q"] is not None:
            free[o["q"]] = t0 + o["cost"]
        for j in succ[i]:
            late = ops[j]["deps"][i] or ops[j]["q"] is None or o["q"] is None
            at[j] = max(at[j], t0 + o["cost"] + (o["lat"] + OPT["hop"] if late else 0.0))
            left[j] -= 1
            if left[j] == 0:
                ready[ops[j]["q"]].append(j)

    total, token = {}, {}
    for i in order:
        o = ops[i]
        name, step = o["sem"] or (COUNTER[o["q"]], 1)
        total[name] = total.get(name, 0) + step * len(o["fn"])
        token[i] = (name, total[name], step)
    seen, full = {}, {}
    for i in order:
        o = ops[i]
        q = o["q"]
        if q is None:
            continue
        want = {}
        for d, wait in o["deps"].items():
            if wait:
                sem, val, _s = token[d]
                want[sem] = max(want.get(sem, 0), val if ops[d]["sem"] is None else total[sem])
        for sem, val in want.items():
            if seen.get((q, sem), 0) < val:
                queue[q].wait_ge(T.sem[sem], val)
                seen[(q, sem)] = val
                full[sem] = max(full.get(sem, 0), val)
        for fn in o["fn"]:
            ins = fn()
            if token[i][0] != "sent":
                ins.then_inc(T.sem[token[i][0]], token[i][2])
    for sem, val in total.items():
        if full.get(sem, 0) < val:
            g.wait_ge(T.sem[sem], val)
